import numpy as np
import ml_dtypes


def mxq(x, axis, fmt="e4m3"):
    dtype, down = {"e4m3": (ml_dtypes.float8_e4m3fn, 7), "e5m2": (ml_dtypes.float8_e5m2, 14)}[fmt]
    v = np.moveaxis(np.asarray(x, np.float32).astype(ml_dtypes.bfloat16).astype(np.float64), axis, -1)
    blocks = v.reshape(v.shape[:-1] + (-1, 32))
    amax = np.abs(blocks).max(-1, keepdims=True)
    byte = np.maximum(np.where(amax > 0, np.frexp(amax)[1] - 1 + 127, 0) - down, 1)
    scale = np.exp2(byte - 127.0)
    codes = (blocks / scale).astype(np.float32).astype(dtype).astype(np.float64)
    return np.moveaxis((codes * scale).reshape(v.shape), -1, axis)


WIDE = False


def mx_kscale(k):
    if not WIDE:
        return np.ones(k)
    levels = np.array([10, -10, 5, -5, 0])
    if k % 512:
        return np.exp2(np.random.permutation(np.resize(levels, k // 32))).repeat(32)
    a = np.empty((k // 512, 16))
    for p in range(k // 512):
        a[p, :8] = np.random.permutation(np.resize(levels, 8))
        for g in range(8):
            far = levels[np.abs(levels - a[p, g]) >= 10]
            a[p, g + 8] = far[np.random.randint(len(far))]
    return np.exp2(a.ravel()).repeat(32)


def f64(x):
    return np.asarray(x).astype(np.float64)


def striped(idx):
    return np.tile(idx.reshape(-1, 16).T, (8, 1)).astype(np.uint16)


def unstriped(offs):
    return offs[:16].T.reshape(-1).astype(np.int64)


def sigmoid(v):
    return 1.0 / (1.0 + np.exp(-np.maximum(v, -700.0)))


K, T, E, C, H, N = 512, 768, 4, 128, 512, 384


def by_expert(wq, xq):
    return np.concatenate([wq[e].T @ xq[:, e * C:(e + 1) * C] for e in range(E)], axis=1)


def setup_inputs():
    n = np.random.standard_normal
    s = mx_kscale(K)[:, None]
    u = mx_kscale(H)
    return {
        "xT": (n((K, T)) * s).astype(np.float32),
        "w1": (n((E + 1, K, H)) / np.sqrt(K) / s[None]).astype(np.float32),
        "w3": (n((E + 1, K, H)) / np.sqrt(K) / s[None] * u[None, None, :]).astype(np.float32),
        "w2": (n((E + 1, H, N)) / np.sqrt(H) / u[None, :, None]).astype(np.float32),
        "gate": np.tile(np.random.uniform(0.2, 1.0, E * C), (N, 1)).astype(np.float32),
        "offs": striped(np.random.permutation(T)[:E * C]),
    }


def reference(xT, w1, w3, w2, gate, offs):
    idx = unstriped(offs)
    w1q, w3q, w2q = mxq(f64(w1), 1, "e4m3"), mxq(f64(w3), 1, "e4m3"), mxq(f64(w2), 1, "e4m3")
    xs = mxq(f64(xT), 0, "e4m3")
    hs = sigmoid(w1q[E].T @ xs) * (w3q[E].T @ xs)
    ys = w2q[E].T @ mxq(hs, 0, "e4m3")
    xq = mxq(f64(xT)[:, idx], 0, "e4m3")
    h = sigmoid(by_expert(w1q, xq))
    h = h * by_expert(w3q, xq)
    y = by_expert(w2q, mxq(h, 0, "e4m3"))
    out = ys
    out[:, idx] += f64(gate) * y
    return out

@@ -1,0 +1,208 @@
+import concourse.mybir as mybir
+
+FLOPS = 1845493760
+
+K, T, E, C, H, N = 512, 768, 4, 128, 512, 384
+S = E * C
+P = 128
+J = 4
+NT = N // P
+SHARED = E
+
+F32 = mybir.dt.float32
+BF16 = mybir.dt.bfloat16
+U32 = mybir.dt.uint32
+U16 = mybir.dt.uint16
+U8 = mybir.dt.uint8
+FP8X4 = mybir.dt.float8_e4m3fn_x4
+SIGMOID = mybir.ActivationFunctionType.Sigmoid
+MULT = mybir.AluOpType.mult
+ADD = mybir.AluOpType.add
+
+
+def tile_moe_shr_glu_sigmoid_kernel(tc, xT, w1, w3, w2, gate, offs, out):
+    nc = tc.nc
+    with (
+        tc.tile_pool(name="keep", bufs=1) as keep,
+        tc.tile_pool(name="raws", bufs=1) as raws,
+        tc.tile_pool(name="ring", bufs=1) as ring,
+        tc.psum_pool(name="psum", bufs=1) as psum,
+    ):
+        offsets = keep.tile([P, S // 16], U16, name="offsets")
+        nc.sync.dma_start(offsets[:], offs)
+
+        warm = keep.tile([P, 1], F32, name="warm")
+        warm_out = keep.tile([P, 1], F32, name="warm_out")
+        nc.vector.memset(warm[:], 0.0)
+        nc.scalar.activation(warm_out[:], warm[:], SIGMOID)
+
+        windows = []
+        for m in range(NT):
+            window = keep.tile([P, T], F32, name=f"window{m}")
+            nc.gpsimd.memset(window[:], 0.0)
+            windows.append(window)
+
+        x_view = xT.rearrange("(p j) t -> p j t", j=J)
+        x_raw = []
+        for u in range(2):
+            raw = keep.tile([P, 2, T], F32, name=f"x_raw{u}")
+            nc.sync.dma_start(raw[:], x_view[:, 2 * u : 2 * u + 2, :])
+            x_raw.append(raw)
+
+        raw13 = {}
+        raw2 = {}
+
+        def load13(e):
+            for which, w in ((1, w1), (3, w3)):
+                raw = raws.tile([P, J, H], F32, name="raw13", bufs=7)
+                nc.sync.dma_start(raw[:], w[e, :, :].rearrange("(p j) h -> p j h", j=J))
+                raw13[e, which] = raw
+
+        def load2(e):
+            raw = raws.tile([P, J, N], F32, name="raw2", bufs=4)
+            nc.sync.dma_start(raw[:], w2[e, :, :].rearrange("(p j) n -> p j n", j=J))
+            raw2[e] = (raw[:, :, 0:256], raw[:, :, 256:384])
+
+        load13(SHARED)
+        for e in range(E):
+            load13(e)
+            if e == 0:
+                gates = keep.tile([P, NT, S], F32, name="gates")
+                nc.sync.dma_start(gates[:], gate.rearrange("(m p) s -> p m s", p=P))
+            load2(e)
+        last_a = raws.tile([P, J, 256], F32, name="last_a")
+        last_b = raws.tile([P, J, 128], F32, name="last_b")
+        nc.sync.dma_start(last_a[:], w2[SHARED, :, 0:256].rearrange("(p j) n -> p j n", j=J))
+        nc.sync.dma_start(last_b[:], w2[SHARED, :, 256:384].rearrange("(p j) n -> p j n", j=J))
+        raw2[SHARED] = (last_a[:], last_b[:])
+
+        def quantize(name, grouped, width, codes=None, scales=None):
+            if codes is None:
+                codes_t = keep.tile([P, width], U32, name=f"{name}_codes", align_bytes=64)
+                scales_t = keep.tile([P, width], U8, name=f"{name}_scales", align_bytes=64)
+                codes, scales = codes_t[:], scales_t[:]
+            nc.vector.quantize_mx(out=codes.bitcast(FP8X4), scales=scales, in_=grouped)
+            return codes, scales
+
+        def copy(engine, dst, src):
+            if engine == "s":
+                nc.scalar.copy(dst, src)
+            else:
+                nc.vector.tensor_copy(dst, src)
+
+        pairs = []
+        gathered = keep.tile([P, S * J], BF16, name="gathered", align_bytes=64)
+        gathered_words = gathered[:].bitcast(U32).rearrange("p (s u) -> p s u", u=2)
+        tokens = keep.tile([P, T * J], BF16, name="tokens", align_bytes=64)
+        for u, engine in ((0, "v"), (1, "s")):
+            pair = keep.tile([P, T * 2], BF16, name=f"pair{u}", align_bytes=64)
+            copy(engine, pair[:].rearrange("p (t i) -> p t i", i=2), x_raw[u][:].rearrange("p i t -> p t i"))
+            pairs.append(pair)
+        for u in range(2):
+            nc.vector.tensor_copy(gathered_words[:, :, u], pairs[u][:].bitcast(U32).indirect(offsets[:]))
+            if u == 0:
+                xs_codes = keep.tile([P, T], U32, name="xs_codes", align_bytes=64)
+                xs_scales = keep.tile([P, T], U8, name="xs_scales", align_bytes=64)
+        for u in range(2):
+            copy(
+                "vs"[u],
+                tokens[:].rearrange("p (t u i) -> p t u i", u=2, i=2)[:, :, u, :],
+                x_raw[u][:].rearrange("p i t -> p t i"),
+            )
+        quantize("xs", tokens[:, 0:2048], 512, xs_codes[:, 0:512], xs_scales[:, 0:512])
+        quantize("xs", tokens[:, 2048:3072], 256, xs_codes[:, 512:768], xs_scales[:, 512:768])
+        xg_codes, xg_scales = quantize("xg", gathered[:], S)
+
+        wq = {}
+
+        def prepare13(e, which, engines):
+            raw = raw13[e, which]
+            grouped = ring.tile([P, H * J], BF16, name="grouped", bufs=5, align_bytes=64)
+            step = J // len(engines)
+            for i, engine in enumerate(engines):
+                copy(
+                    engine,
+                    grouped[:].rearrange("p (t m j) -> p m j t", t=J, j=J)[:, :, :, i * step : i * step + step],
+                    raw[:].rearrange("p j (m t) -> p m j t", t=J)[:, :, :, i * step : i * step + step],
+                )
+            wq[e, which] = quantize(f"w{which}_{e}", grouped[:], H)
+
+        def prepare2(e, engines):
+            parts = []
+            for s, width in ((0, 256), (1, 128)):
+                grouped = ring.tile([P, 1024], BF16, name="grouped2", bufs=6, align_bytes=64)
+                copy(
+                    engines[s],
+                    grouped[:, 0 : width * J].rearrange("p (c i j) -> p c j i", i=4, j=J),
+                    raw2[e][s].rearrange("p j (c i) -> p c j i", i=4),
+                )
+                parts.append(quantize(f"w2_{e}_{s}", grouped[:, 0 : width * J], width))
+            wq[e, 2] = parts
+
+        def matmul(dst, part, column, codes, scales):
+            nc.tensor.matmul_mx(
+                out=dst,
+                lhsT=part[0][:, column : column + P].bitcast(FP8X4),
+                lhsT_scale=part[1][:, column : column + P],
+                rhs=codes.bitcast(FP8X4),
+                rhs_scale=scales,
+                start=True,
+                stop=True,
+            )
+
+        h_codes = keep.tile([P, S], U32, name="h_codes", align_bytes=64)
+        h_scales = keep.tile([P, S], U8, name="h_scales", align_bytes=64)
+        hs_codes = keep.tile([P, T], U32, name="hs_codes", align_bytes=64)
+        hs_scales = keep.tile([P, T], U8, name="hs_scales", align_bytes=64)
+
+        def first_layer(e, chunk, x_codes, x_scales, y_codes, y_scales):
+            cols = slice(chunk * C, chunk * C + C)
+            banks = []
+            for which, tag in ((1, "bank_a"), (3, "bank_b")):
+                bank = psum.tile([P, J, C], F32, name=tag, bufs=2)
+                for t in range(J):
+                    matmul(bank[:, t, :], wq[e, which], t * P, x_codes[:, cols], x_scales[:, cols])
+                banks.append(bank)
+            sig = ring.tile([P, C, J], F32, name="sig", bufs=3)
+            nc.scalar.activation(sig[:], banks[0][:].rearrange("p t n -> p n t"), SIGMOID)
+            hidden = ring.tile([P, C, J], BF16, name="hidden", bufs=3, align_bytes=64)
+            nc.vector.tensor_tensor(hidden[:], banks[1][:].rearrange("p t n -> p n t"), sig[:], MULT)
+            quantize("h", hidden[:].rearrange("p n t -> p (n t)"), C, y_codes[:, cols], y_scales[:, cols])
+
+        def shared_chunk(chunk):
+            first_layer(SHARED, chunk, xs_codes[:], xs_scales[:], hs_codes[:], hs_scales[:])
+
+        prepare13(SHARED, 1, "s")
+        prepare13(SHARED, 3, "sv")
+        for e in range(E):
+            if e < 3:
+                shared_chunk(2 * e)
+                shared_chunk(2 * e + 1)
+            prepare13(e, 1, "s")
+            prepare13(e, 3, "sv")
+            first_layer(e, e, xg_codes, xg_scales, h_codes[:], h_scales[:])
+            prepare2(e, "sv")
+            cols = slice(e * C, e * C + C)
+            bank = psum.tile([P, 512], F32, name="bank_o", bufs=4)
+            for m in range(NT):
+                matmul(bank[:, m * P : m * P + P], wq[e, 2][m // 2], (m % 2) * P, h_codes[:, cols], h_scales[:, cols])
+            routed = ring.tile([P, N], F32, name="routed", bufs=3)
+            nc.vector.tensor_tensor(
+                routed[:].rearrange("p (m s) -> p m s", m=NT),
+                bank[:, 0:N].rearrange("p (m s) -> p m s", m=NT),
+                gates[:, :, cols],
+                MULT,
+            )
+            for m in range(NT):
+                nc.vector.tensor_copy(
+                    windows[m][:].indirect(offsets[:, e * 8 : e * 8 + 8]), routed[:, m * P : m * P + P]
+                )
+
+        prepare2(SHARED, "sv")
+        for m in range(NT):
+            result = ring.tile([P, T], F32, name="result", bufs=3)
+            for t0, t1 in ((0, 512), (512, 768)):
+                bank = psum.tile([P, 512], F32, name="bank_o", bufs=4)
+                matmul(bank[:, 0 : t1 - t0], wq[SHARED, 2][m // 2], (m % 2) * P, hs_codes[:, t0:t1], hs_scales[:, t0:t1])
+                nc.vector.tensor_tensor(result[:, t0:t1], bank[:, 0 : t1 - t0], windows[m][:, t0:t1], ADD)
+            nc.sync.dma_start(out[m * P : m * P + P, :], result[:])

@@ -187,15 +187,13 @@ def tile_moe_shr_glu_sigmoid_kernel(tc, xT, w1, w3, w2, gate, offs, out):
             for m in range(NT):
                 matmul(bank[:, m * P : m * P + P], wq[e, 2][m // 2], (m % 2) * P, h_codes[:, cols], h_scales[:, cols])
             routed = ring.tile([P, N], F32, name="routed", bufs=3)
-            nc.vector.tensor_tensor(
-                routed[:].rearrange("p (m s) -> p m s", m=NT),
-                bank[:, 0:N].rearrange("p (m s) -> p m s", m=NT),
-                gates[:, :, cols],
-                MULT,
-            )
+            nc.scalar.copy(routed[:], bank[:, 0:N])
             for m in range(NT):
-                nc.vector.tensor_copy(
-                    windows[m][:].indirect(offsets[:, e * 8 : e * 8 + 8]), routed[:, m * P : m * P + P]
+                nc.vector.tensor_tensor(
+                    windows[m][:].indirect(offsets[:, e * 8 : e * 8 + 8]),
+                    routed[:, m * P : m * P + P],
+                    gates[:, m, cols],
+                    MULT,
                 )
 
         prepare2(SHARED, "sv")

@@ -19,6 +19,9 @@ SIGMOID = mybir.ActivationFunctionType.Sigmoid
 MULT = mybir.AluOpType.mult
 ADD = mybir.AluOpType.add
 
+S13 = (64, 80, 80, 88, 88)
+S2 = (256, 256, 256, 256, 256)
+
 
 def tile_moe_shr_glu_sigmoid_kernel(tc, xT, w1, w3, w2, gate, offs, out):
     nc = tc.nc
@@ -28,13 +31,22 @@ def tile_moe_shr_glu_sigmoid_kernel(tc, xT, w1, w3, w2, gate, offs, out):
         tc.tile_pool(name="ring", bufs=1) as ring,
         tc.psum_pool(name="psum", bufs=1) as psum,
     ):
-        offsets = keep.tile([P, S // 16], U16, name="offsets")
-        nc.sync.dma_start(offsets[:], offs)
-
         warm = keep.tile([P, 1], F32, name="warm")
         warm_out = keep.tile([P, 1], F32, name="warm_out")
         nc.vector.memset(warm[:], 0.0)
         nc.scalar.activation(warm_out[:], warm[:], SIGMOID)
+
+        offsets = keep.tile([P, S // 16], U16, name="offsets")
+        x_view = xT.rearrange("(p j) t -> p j t", j=J)
+        x_raw = []
+        halves = (slice(0, T // 2), slice(T // 2, T))
+        for u in range(2):
+            for half in halves:
+                raw = keep.tile([P, 2, T // 2], F32, name=f"x_raw{len(x_raw)}")
+                nc.sync.dma_start(raw[:], x_view[:, 2 * u : 2 * u + 2, half])
+                x_raw.append(raw)
+            if u == 0:
+                nc.sync.dma_start(offsets[:], offs)
 
         windows = []
         for m in range(NT):
@@ -42,121 +54,101 @@ def tile_moe_shr_glu_sigmoid_kernel(tc, xT, w1, w3, w2, gate, offs, out):
             nc.gpsimd.memset(window[:], 0.0)
             windows.append(window)
 
-        x_view = xT.rearrange("(p j) t -> p j t", j=J)
-        x_raw = []
-        for u in range(2):
-            raw = keep.tile([P, 2, T], F32, name=f"x_raw{u}")
-            nc.sync.dma_start(raw[:], x_view[:, 2 * u : 2 * u + 2, :])
-            x_raw.append(raw)
-
-        raw13 = {}
-        raw2 = {}
+        raw_w = {}
 
         def load13(e):
             for which, w in ((1, w1), (3, w3)):
                 raw = raws.tile([P, J, H], F32, name="raw13", bufs=7)
                 nc.sync.dma_start(raw[:], w[e, :, :].rearrange("(p j) h -> p j h", j=J))
-                raw13[e, which] = raw
+                raw_w[e, which] = raw
 
         def load2(e):
             raw = raws.tile([P, J, N], F32, name="raw2", bufs=4)
             nc.sync.dma_start(raw[:], w2[e, :, :].rearrange("(p j) n -> p j n", j=J))
-            raw2[e] = (raw[:, :, 0:256], raw[:, :, 256:384])
+            raw_w[e, 2] = raw
 
+        gates = keep.tile([P, NT, S], F32, name="gates")
         load13(SHARED)
         for e in range(E):
             load13(e)
             if e == 0:
-                gates = keep.tile([P, NT, S], F32, name="gates")
                 nc.sync.dma_start(gates[:], gate.rearrange("(m p) s -> p m s", p=P))
             load2(e)
-        last_a = raws.tile([P, J, 256], F32, name="last_a")
-        last_b = raws.tile([P, J, 128], F32, name="last_b")
-        nc.sync.dma_start(last_a[:], w2[SHARED, :, 0:256].rearrange("(p j) n -> p j n", j=J))
-        nc.sync.dma_start(last_b[:], w2[SHARED, :, 256:384].rearrange("(p j) n -> p j n", j=J))
-        raw2[SHARED] = (last_a[:], last_b[:])
+        load2(SHARED)
 
-        def quantize(name, grouped, width, codes=None, scales=None):
-            if codes is None:
-                codes_t = keep.tile([P, width], U32, name=f"{name}_codes", align_bytes=64)
-                scales_t = keep.tile([P, width], U8, name=f"{name}_scales", align_bytes=64)
-                codes, scales = codes_t[:], scales_t[:]
+        def quantize(grouped, codes, scales):
             nc.vector.quantize_mx(out=codes.bitcast(FP8X4), scales=scales, in_=grouped)
+
+        def quantized(name, width):
+            codes = keep.tile([P, width], U32, name=f"{name}_codes", align_bytes=64)
+            scales = keep.tile([P, width], U8, name=f"{name}_scales", align_bytes=64)
             return codes, scales
 
-        def copy(engine, dst, src):
-            if engine == "s":
-                nc.scalar.copy(dst, src)
-            else:
-                nc.vector.tensor_copy(dst, src)
-
-        pairs = []
+        pairs = keep.tile([P, 2, T, 2], BF16, name="pairs", align_bytes=64)
         gathered = keep.tile([P, S * J], BF16, name="gathered", align_bytes=64)
-        gathered_words = gathered[:].bitcast(U32).rearrange("p (s u) -> p s u", u=2)
         tokens = keep.tile([P, T * J], BF16, name="tokens", align_bytes=64)
-        for u, engine in ((0, "v"), (1, "s")):
-            pair = keep.tile([P, T * 2], BF16, name=f"pair{u}", align_bytes=64)
-            copy(engine, pair[:].rearrange("p (t i) -> p t i", i=2), x_raw[u][:].rearrange("p i t -> p t i"))
-            pairs.append(pair)
+        xg_codes, xg_scales = quantized("xg", S)
+        xs_codes, xs_scales = quantized("xs", T)
         for u in range(2):
-            nc.vector.tensor_copy(gathered_words[:, :, u], pairs[u][:].bitcast(U32).indirect(offsets[:]))
-            if u == 0:
-                xs_codes = keep.tile([P, T], U32, name="xs_codes", align_bytes=64)
-                xs_scales = keep.tile([P, T], U8, name="xs_scales", align_bytes=64)
-        for u in range(2):
-            copy(
-                "vs"[u],
-                tokens[:].rearrange("p (t u i) -> p t u i", u=2, i=2)[:, :, u, :],
-                x_raw[u][:].rearrange("p i t -> p t i"),
+            for i, half in enumerate(halves):
+                dst, src = pairs[:, u, half, :], x_raw[2 * u + i][:].rearrange("p i t -> p t i")
+                if i == 0:
+                    nc.vector.tensor_copy(dst, src)
+                else:
+                    nc.scalar.copy(dst, src)
+            words = pairs[:, u, :, :].rearrange("p t i -> p (t i)").bitcast(U32)
+            nc.vector.tensor_copy(
+                gathered[:].bitcast(U32).rearrange("p (s u) -> p s u", u=2)[:, :, u], words.indirect(offsets[:])
             )
-        quantize("xs", tokens[:, 0:2048], 512, xs_codes[:, 0:512], xs_scales[:, 0:512])
-        quantize("xs", tokens[:, 2048:3072], 256, xs_codes[:, 512:768], xs_scales[:, 512:768])
-        xg_codes, xg_scales = quantize("xg", gathered[:], S)
+        nc.vector.tensor_copy(
+            tokens[:].bitcast(F32).rearrange("p (t u) -> p t u", u=2),
+            pairs[:].rearrange("p u t i -> p (u t i)").bitcast(F32).rearrange("p (u t) -> p t u", u=2),
+        )
+        for t0, t1 in ((0, 512), (512, 768)):
+            quantize(tokens[:, t0 * J : t1 * J], xs_codes[:, t0:t1], xs_scales[:, t0:t1])
+        quantize(gathered[:], xg_codes[:], xg_scales[:])
 
         wq = {}
 
-        def prepare13(e, which, engines):
-            raw = raw13[e, which]
-            grouped = ring.tile([P, H * J], BF16, name="grouped", bufs=5, align_bytes=64)
-            step = J // len(engines)
-            for i, engine in enumerate(engines):
-                copy(
-                    engine,
-                    grouped[:].rearrange("p (t m j) -> p m j t", t=J, j=J)[:, :, :, i * step : i * step + step],
-                    raw[:].rearrange("p j (m t) -> p m j t", t=J)[:, :, :, i * step : i * step + step],
-                )
-            wq[e, which] = quantize(f"w{which}_{e}", grouped[:], H)
+        def prepare13(e, which):
+            grouped = ring.tile([P, H * J], BF16, name="grouped13", bufs=5, align_bytes=64)
+            dst = grouped[:].rearrange("p (t m j) -> p m j t", t=J, j=J)
+            src = raw_w[e, which][:].rearrange("p j (m t) -> p m j t", t=J)
+            cut = S13[e]
+            nc.scalar.copy(dst[:, 0:cut], src[:, 0:cut])
+            if cut < P:
+                nc.vector.tensor_copy(dst[:, cut:P], src[:, cut:P])
+            wq[e, which] = quantized(f"w{which}_{e}", H)
+            quantize(grouped[:], wq[e, which][0][:], wq[e, which][1][:])
 
-        def prepare2(e, engines):
-            parts = []
-            for s, width in ((0, 256), (1, 128)):
-                grouped = ring.tile([P, 1024], BF16, name="grouped2", bufs=6, align_bytes=64)
-                copy(
-                    engines[s],
-                    grouped[:, 0 : width * J].rearrange("p (c i j) -> p c j i", i=4, j=J),
-                    raw2[e][s].rearrange("p j (c i) -> p c j i", i=4),
-                )
-                parts.append(quantize(f"w2_{e}_{s}", grouped[:, 0 : width * J], width))
-            wq[e, 2] = parts
+        def prepare2(e):
+            grouped = ring.tile([P, N * J], BF16, name="grouped2", bufs=4, align_bytes=64)
+            dst = grouped[:].rearrange("p (c i j) -> p c j i", i=4, j=J)
+            src = raw_w[e, 2][:].rearrange("p j (c i) -> p c j i", i=4)
+            cut = S2[e] // 4
+            if cut > 0:
+                nc.scalar.copy(dst[:, 0:cut], src[:, 0:cut])
+            if cut < N // 4:
+                nc.vector.tensor_copy(dst[:, cut : N // 4], src[:, cut : N // 4])
+            wq[e, 2] = quantized(f"w2_{e}", N)
+            for n0, n1 in ((0, 256), (256, 384)):
+                quantize(grouped[:, n0 * J : n1 * J], wq[e, 2][0][:, n0:n1], wq[e, 2][1][:, n0:n1])
 
-        def matmul(dst, part, column, codes, scales):
+        def matmul(dst, weights, column, codes, scales):
             nc.tensor.matmul_mx(
                 out=dst,
-                lhsT=part[0][:, column : column + P].bitcast(FP8X4),
-                lhsT_scale=part[1][:, column : column + P],
+                lhsT=weights[0][:, column : column + P].bitcast(FP8X4),
+                lhsT_scale=weights[1][:, column : column + P],
                 rhs=codes.bitcast(FP8X4),
                 rhs_scale=scales,
                 start=True,
                 stop=True,
             )
 
-        h_codes = keep.tile([P, S], U32, name="h_codes", align_bytes=64)
-        h_scales = keep.tile([P, S], U8, name="h_scales", align_bytes=64)
-        hs_codes = keep.tile([P, T], U32, name="hs_codes", align_bytes=64)
-        hs_scales = keep.tile([P, T], U8, name="hs_scales", align_bytes=64)
+        h_codes, h_scales = quantized("h", S)
+        hs_codes, hs_scales = quantized("hs", T)
 
-        def first_layer(e, chunk, x_codes, x_scales, y_codes, y_scales):
-            cols = slice(chunk * C, chunk * C + C)
+        def first_layer(e, cols, x_codes, x_scales, hidden):
             banks = []
             for which, tag in ((1, "bank_a"), (3, "bank_b")):
                 bank = psum.tile([P, J, C], F32, name=tag, bufs=2)
@@ -165,42 +157,55 @@ def tile_moe_shr_glu_sigmoid_kernel(tc, xT, w1, w3, w2, gate, offs, out):
                 banks.append(bank)
             sig = ring.tile([P, C, J], F32, name="sig", bufs=3)
             nc.scalar.activation(sig[:], banks[0][:].rearrange("p t n -> p n t"), SIGMOID)
-            hidden = ring.tile([P, C, J], BF16, name="hidden", bufs=3, align_bytes=64)
-            nc.vector.tensor_tensor(hidden[:], banks[1][:].rearrange("p t n -> p n t"), sig[:], MULT)
-            quantize("h", hidden[:].rearrange("p n t -> p (n t)"), C, y_codes[:, cols], y_scales[:, cols])
+            nc.vector.tensor_tensor(
+                hidden.rearrange("p (n t) -> p n t", t=J), banks[1][:].rearrange("p t n -> p n t"), sig[:], MULT
+            )
 
-        def shared_chunk(chunk):
-            first_layer(SHARED, chunk, xs_codes[:], xs_scales[:], hs_codes[:], hs_scales[:])
+        def shared_chunk(pair):
+            hidden = ring.tile([P, 2 * C * J], BF16, name="hidden_s", bufs=2, align_bytes=64)
+            for i in range(2):
+                chunk = 2 * pair + i
+                cols = slice(chunk * C, chunk * C + C)
+                first_layer(SHARED, cols, xs_codes, xs_scales, hidden[:, i * C * J : (i + 1) * C * J])
+            cols = slice(pair * 2 * C, (pair + 1) * 2 * C)
+            quantize(hidden[:], hs_codes[:, cols], hs_scales[:, cols])
 
-        prepare13(SHARED, 1, "s")
-        prepare13(SHARED, 3, "sv")
-        for e in range(E):
-            if e < 3:
-                shared_chunk(2 * e)
-                shared_chunk(2 * e + 1)
-            prepare13(e, 1, "s")
-            prepare13(e, 3, "sv")
-            first_layer(e, e, xg_codes, xg_scales, h_codes[:], h_scales[:])
-            prepare2(e, "sv")
+        def routed_first(e):
+            cols = slice(e * C, e * C + C)
+            hidden = ring.tile([P, C * J], BF16, name="hidden_r", bufs=2, align_bytes=64)
+            first_layer(e, cols, xg_codes, xg_scales, hidden[:])
+            quantize(hidden[:], h_codes[:, cols], h_scales[:, cols])
+
+        def routed_second(e):
             cols = slice(e * C, e * C + C)
             bank = psum.tile([P, 512], F32, name="bank_o", bufs=4)
             for m in range(NT):
-                matmul(bank[:, m * P : m * P + P], wq[e, 2][m // 2], (m % 2) * P, h_codes[:, cols], h_scales[:, cols])
-            routed = ring.tile([P, N], F32, name="routed", bufs=3)
-            nc.scalar.copy(routed[:], bank[:, 0:N])
+                matmul(bank[:, m * P : m * P + P], wq[e, 2], m * P, h_codes[:, cols], h_scales[:, cols])
+            routed = ring.tile([P, NT, C], F32, name="routed", bufs=3)
+            nc.scalar.copy(routed[:].rearrange("p m s -> p (m s)"), bank[:, 0:N])
             for m in range(NT):
                 nc.vector.tensor_tensor(
-                    windows[m][:].indirect(offsets[:, e * 8 : e * 8 + 8]),
-                    routed[:, m * P : m * P + P],
-                    gates[:, m, cols],
-                    MULT,
+                    windows[m][:].indirect(offsets[:, e * 8 : e * 8 + 8]), routed[:, m, :], gates[:, m, cols], MULT
                 )
 
-        prepare2(SHARED, "sv")
-        for m in range(NT):
-            result = ring.tile([P, T], F32, name="result", bufs=3)
-            for t0, t1 in ((0, 512), (512, 768)):
-                bank = psum.tile([P, 512], F32, name="bank_o", bufs=4)
-                matmul(bank[:, 0 : t1 - t0], wq[SHARED, 2][m // 2], (m % 2) * P, hs_codes[:, t0:t1], hs_scales[:, t0:t1])
-                nc.vector.tensor_tensor(result[:, t0:t1], bank[:, 0 : t1 - t0], windows[m][:, t0:t1], ADD)
-            nc.sync.dma_start(out[m * P : m * P + P, :], result[:])
+        def shared_second():
+            for m in range(NT):
+                result = ring.tile([P, T], F32, name="result", bufs=3)
+                for t0, t1 in ((0, 512), (512, 768)):
+                    bank = psum.tile([P, 512], F32, name="bank_o", bufs=4)
+                    matmul(bank[:, 0 : t1 - t0], wq[SHARED, 2], m * P, hs_codes[:, t0:t1], hs_scales[:, t0:t1])
+                    nc.vector.tensor_tensor(result[:, t0:t1], bank[:, 0 : t1 - t0], windows[m][:, t0:t1], ADD)
+                nc.sync.dma_start(out[m * P : m * P + P, :], result[:])
+
+        prepare13(SHARED, 1)
+        prepare13(SHARED, 3)
+        for e in range(E):
+            prepare13(e, 1)
+            prepare13(e, 3)
+            if e < 3:
+                shared_chunk(e)
+            routed_first(e)
+            prepare2(e)
+            routed_second(e)
+        prepare2(SHARED)
+        shared_second()

@@ -19,8 +19,10 @@ SIGMOID = mybir.ActivationFunctionType.Sigmoid
 MULT = mybir.AluOpType.mult
 ADD = mybir.AluOpType.add
 
-S13 = (64, 80, 80, 88, 88)
-S2 = (256, 256, 256, 256, 256)
+UNITS = ((4, 1), (4, 3), (0, 3), (0, 1), (1, 1), (0, 2), (1, 3), (1, 2), (2, 3), (2, 1), (3, 1), (3, 3), (2, 2), (3, 2), (4, 2))
+GATE_AFTER = (2, 3)
+S8 = (5, 4, 4, 2, 2, 5, 5, 3, 8, 6, 5, 4, 6, 8, 8)
+CHUNK_STEPS = (3, 4, 6, 7, 9, 13)
 
 
 def tile_moe_shr_glu_sigmoid_kernel(tc, xT, w1, w3, w2, gate, offs, out):
@@ -54,27 +56,18 @@ def tile_moe_shr_glu_sigmoid_kernel(tc, xT, w1, w3, w2, gate, offs, out):
             nc.gpsimd.memset(window[:], 0.0)
             windows.append(window)
 
-        raw_w = {}
-
-        def load13(e):
-            for which, w in ((1, w1), (3, w3)):
-                raw = raws.tile([P, J, H], F32, name="raw13", bufs=7)
-                nc.sync.dma_start(raw[:], w[e, :, :].rearrange("(p j) h -> p j h", j=J))
-                raw_w[e, which] = raw
-
-        def load2(e):
-            raw = raws.tile([P, J, N], F32, name="raw2", bufs=4)
-            nc.sync.dma_start(raw[:], w2[e, :, :].rearrange("(p j) n -> p j n", j=J))
-            raw_w[e, 2] = raw
-
         gates = keep.tile([P, NT, S], F32, name="gates")
-        load13(SHARED)
-        for e in range(E):
-            load13(e)
-            if e == 0:
+        raw_w = {}
+        for e, layer in UNITS:
+            if layer == 2:
+                raw = raws.tile([P, J, N], F32, name="raw2", bufs=4)
+            else:
+                raw = raws.tile([P, J, H], F32, name="raw13", bufs=7)
+            source = {1: w1, 3: w3, 2: w2}[layer]
+            nc.sync.dma_start(raw[:], source[e, :, :].rearrange("(p j) c -> p j c", j=J))
+            raw_w[e, layer] = raw
+            if (e, layer) == GATE_AFTER:
                 nc.sync.dma_start(gates[:], gate.rearrange("(m p) s -> p m s", p=P))
-            load2(e)
-        load2(SHARED)
 
         def quantize(grouped, codes, scales):
             nc.vector.quantize_mx(out=codes.bitcast(FP8X4), scales=scales, in_=grouped)
@@ -92,7 +85,7 @@ def tile_moe_shr_glu_sigmoid_kernel(tc, xT, w1, w3, w2, gate, offs, out):
         for u in range(2):
             for i, half in enumerate(halves):
                 dst, src = pairs[:, u, half, :], x_raw[2 * u + i][:].rearrange("p i t -> p t i")
-                if i == 0:
+                if "AVAA"[2 * u + i] == "V":
                     nc.vector.tensor_copy(dst, src)
                 else:
                     nc.scalar.copy(dst, src)
@@ -100,39 +93,48 @@ def tile_moe_shr_glu_sigmoid_kernel(tc, xT, w1, w3, w2, gate, offs, out):
             nc.vector.tensor_copy(
                 gathered[:].bitcast(U32).rearrange("p (s u) -> p s u", u=2)[:, :, u], words.indirect(offsets[:])
             )
-        nc.vector.tensor_copy(
+        nc.scalar.copy(
             tokens[:].bitcast(F32).rearrange("p (t u) -> p t u", u=2),
             pairs[:].rearrange("p u t i -> p (u t i)").bitcast(F32).rearrange("p (u t) -> p t u", u=2),
         )
+        quantize(gathered[:], xg_codes[:], xg_scales[:])
         for t0, t1 in ((0, 512), (512, 768)):
             quantize(tokens[:, t0 * J : t1 * J], xs_codes[:, t0:t1], xs_scales[:, t0:t1])
-        quantize(gathered[:], xg_codes[:], xg_scales[:])
 
-        wq = {}
+        wq, views = {}, {}
 
-        def prepare13(e, which):
-            grouped = ring.tile([P, H * J], BF16, name="grouped13", bufs=5, align_bytes=64)
-            dst = grouped[:].rearrange("p (t m j) -> p m j t", t=J, j=J)
-            src = raw_w[e, which][:].rearrange("p j (m t) -> p m j t", t=J)
-            cut = S13[e]
-            nc.scalar.copy(dst[:, 0:cut], src[:, 0:cut])
-            if cut < P:
-                nc.vector.tensor_copy(dst[:, cut:P], src[:, cut:P])
-            wq[e, which] = quantized(f"w{which}_{e}", H)
-            quantize(grouped[:], wq[e, which][0][:], wq[e, which][1][:])
+        def cast_views(unit):
+            e, layer = unit
+            if layer == 2:
+                grouped = ring.tile([P, N * J], BF16, name="grouped2", bufs=3, align_bytes=64)
+                dst = grouped[:].rearrange("p (c i j) -> p c j i", i=4, j=J)
+                src = raw_w[unit][:].rearrange("p j (c i) -> p c j i", i=4)
+                cut = S8[UNITS.index(unit)] * 12
+            else:
+                grouped = ring.tile([P, H * J], BF16, name="grouped13", bufs=4, align_bytes=64)
+                dst = grouped[:].rearrange("p (t m j) -> p m j t", t=J, j=J)
+                src = raw_w[unit][:].rearrange("p j (m t) -> p m j t", t=J)
+                cut = S8[UNITS.index(unit)] * 16
+            views[unit] = grouped, dst, src, cut
 
-        def prepare2(e):
-            grouped = ring.tile([P, N * J], BF16, name="grouped2", bufs=4, align_bytes=64)
-            dst = grouped[:].rearrange("p (c i j) -> p c j i", i=4, j=J)
-            src = raw_w[e, 2][:].rearrange("p j (c i) -> p c j i", i=4)
-            cut = S2[e] // 4
+        def cast_scalar(unit):
+            cast_views(unit)
+            grouped, dst, src, cut = views[unit]
             if cut > 0:
                 nc.scalar.copy(dst[:, 0:cut], src[:, 0:cut])
-            if cut < N // 4:
-                nc.vector.tensor_copy(dst[:, cut : N // 4], src[:, cut : N // 4])
-            wq[e, 2] = quantized(f"w2_{e}", N)
-            for n0, n1 in ((0, 256), (256, 384)):
-                quantize(grouped[:, n0 * J : n1 * J], wq[e, 2][0][:, n0:n1], wq[e, 2][1][:, n0:n1])
+
+        def cast_vector(unit):
+            grouped, dst, src, cut = views[unit]
+            if cut < dst.shape[1]:
+                nc.vector.tensor_copy(dst[:, cut:], src[:, cut:])
+
+        def quantize_weights(unit):
+            e, layer = unit
+            grouped = views[unit][0]
+            width, cuts = (N, (0, 256, 384)) if layer == 2 else (H, (0, 512))
+            codes, scales = wq[unit] = quantized(f"w{layer}_{e}", width)
+            for n0, n1 in zip(cuts[:-1], cuts[1:]):
+                quantize(grouped[:, n0 * J : n1 * J], codes[:, n0:n1], scales[:, n0:n1])
 
         def matmul(dst, weights, column, codes, scales):
             nc.tensor.matmul_mx(
@@ -147,65 +149,106 @@ def tile_moe_shr_glu_sigmoid_kernel(tc, xT, w1, w3, w2, gate, offs, out):
 
         h_codes, h_scales = quantized("h", S)
         hs_codes, hs_scales = quantized("hs", T)
+        banks, sigs, hiddens = {}, {}, {}
 
-        def first_layer(e, cols, x_codes, x_scales, hidden):
-            banks = []
-            for which, tag in ((1, "bank_a"), (3, "bank_b")):
+        def multiply_first(chunk):
+            e, c = chunk
+            cols = slice(c * C, c * C + C)
+            codes, scales = (xs_codes, xs_scales) if e == SHARED else (xg_codes, xg_scales)
+            for layer, tag in ((1, "bank_a"), (3, "bank_b")):
                 bank = psum.tile([P, J, C], F32, name=tag, bufs=2)
                 for t in range(J):
-                    matmul(bank[:, t, :], wq[e, which], t * P, x_codes[:, cols], x_scales[:, cols])
-                banks.append(bank)
+                    matmul(bank[:, t, :], wq[e, layer], t * P, codes[:, cols], scales[:, cols])
+                banks[chunk, layer] = bank
+
+        def sigmoid(chunk):
             sig = ring.tile([P, C, J], F32, name="sig", bufs=3)
-            nc.scalar.activation(sig[:], banks[0][:].rearrange("p t n -> p n t"), SIGMOID)
+            nc.scalar.activation(sig[:], banks[chunk, 1][:].rearrange("p t n -> p n t"), SIGMOID)
+            sigs[chunk] = sig
+
+        def product(chunk):
+            e, c = chunk
+            if e == SHARED and c % 2 == 1:
+                hidden, at = hiddens[e, c - 1][0], C * J
+            else:
+                width = 2 if e == SHARED else 1
+                hidden, at = ring.tile([P, width * C * J], BF16, name=f"hidden{width}", bufs=2, align_bytes=64), 0
             nc.vector.tensor_tensor(
-                hidden.rearrange("p (n t) -> p n t", t=J), banks[1][:].rearrange("p t n -> p n t"), sig[:], MULT
+                hidden[:, at : at + C * J].rearrange("p (n t) -> p n t", t=J),
+                banks[chunk, 3][:].rearrange("p t n -> p n t"),
+                sigs[chunk][:],
+                MULT,
             )
+            hiddens[chunk] = hidden, at
 
-        def shared_chunk(pair):
-            hidden = ring.tile([P, 2 * C * J], BF16, name="hidden_s", bufs=2, align_bytes=64)
-            for i in range(2):
-                chunk = 2 * pair + i
-                cols = slice(chunk * C, chunk * C + C)
-                first_layer(SHARED, cols, xs_codes, xs_scales, hidden[:, i * C * J : (i + 1) * C * J])
-            cols = slice(pair * 2 * C, (pair + 1) * 2 * C)
-            quantize(hidden[:], hs_codes[:, cols], hs_scales[:, cols])
+        def quantize_hidden(chunk):
+            e, c = chunk
+            if e == SHARED and c % 2 == 0:
+                return
+            first = c - 1 if e == SHARED else c
+            cols = slice(first * C, c * C + C)
+            codes, scales = (hs_codes, hs_scales) if e == SHARED else (h_codes, h_scales)
+            quantize(hiddens[chunk][0][:], codes[:, cols], scales[:, cols])
 
-        def routed_first(e):
-            cols = slice(e * C, e * C + C)
-            hidden = ring.tile([P, C * J], BF16, name="hidden_r", bufs=2, align_bytes=64)
-            first_layer(e, cols, xg_codes, xg_scales, hidden[:])
-            quantize(hidden[:], h_codes[:, cols], h_scales[:, cols])
-
-        def routed_second(e):
+        def multiply_second(e):
             cols = slice(e * C, e * C + C)
             bank = psum.tile([P, 512], F32, name="bank_o", bufs=4)
             for m in range(NT):
                 matmul(bank[:, m * P : m * P + P], wq[e, 2], m * P, h_codes[:, cols], h_scales[:, cols])
-            routed = ring.tile([P, NT, C], F32, name="routed", bufs=3)
-            nc.scalar.copy(routed[:].rearrange("p m s -> p (m s)"), bank[:, 0:N])
+            banks[e] = bank
+
+        routeds = {}
+
+        def copy_routed(e):
+            routed = ring.tile([P, N], F32, name="routed", bufs=2)
+            nc.scalar.copy(routed[:], banks[e][:, 0:N])
+            routeds[e] = routed
+
+        def scatter(e):
             for m in range(NT):
                 nc.vector.tensor_tensor(
-                    windows[m][:].indirect(offsets[:, e * 8 : e * 8 + 8]), routed[:, m, :], gates[:, m, cols], MULT
+                    windows[m][:].indirect(offsets[:, e * 8 : e * 8 + 8]),
+                    routeds[e][:, m * P : m * P + P],
+                    gates[:, m, e * C : e * C + C],
+                    MULT,
                 )
 
-        def shared_second():
-            for m in range(NT):
-                result = ring.tile([P, T], F32, name="result", bufs=3)
-                for t0, t1 in ((0, 512), (512, 768)):
-                    bank = psum.tile([P, 512], F32, name="bank_o", bufs=4)
-                    matmul(bank[:, 0 : t1 - t0], wq[SHARED, 2], m * P, hs_codes[:, t0:t1], hs_scales[:, t0:t1])
-                    nc.vector.tensor_tensor(result[:, t0:t1], bank[:, 0 : t1 - t0], windows[m][:, t0:t1], ADD)
-                nc.sync.dma_start(out[m * P : m * P + P, :], result[:])
-
-        prepare13(SHARED, 1)
-        prepare13(SHARED, 3)
+        step_of = {unit: k for k, unit in enumerate(UNITS)}
+        chunk_step = {(SHARED, c): k for c, k in enumerate(CHUNK_STEPS)}
+        second_step = {}
         for e in range(E):
-            prepare13(e, 1)
-            prepare13(e, 3)
-            if e < 3:
-                shared_chunk(e)
-            routed_first(e)
-            prepare2(e)
-            routed_second(e)
-        prepare2(SHARED)
-        shared_second()
+            chunk_step[e, e] = max(step_of[e, 1], step_of[e, 3]) + 2
+            second_step[e] = max(chunk_step[e, e] + 2, step_of[e, 2] + 2)
+        for k in range(len(UNITS) + 4):
+            started = [chunk for chunk, step in chunk_step.items() if step == k]
+            before = [chunk for chunk, step in chunk_step.items() if step == k - 1]
+            seconds = [e for e, step in second_step.items() if step == k]
+            for e in seconds:
+                multiply_second(e)
+            for chunk in started:
+                multiply_first(chunk)
+            for chunk in before:
+                product(chunk)
+            if k < len(UNITS):
+                cast_scalar(UNITS[k])
+            for e in seconds:
+                copy_routed(e)
+            for chunk in started:
+                sigmoid(chunk)
+            if k < len(UNITS):
+                cast_vector(UNITS[k])
+            if 1 <= k <= len(UNITS):
+                quantize_weights(UNITS[k - 1])
+            for chunk in before:
+                quantize_hidden(chunk)
+            for e, step in second_step.items():
+                if step == k - 1:
+                    scatter(e)
+
+        for m in range(NT):
+            result = ring.tile([P, T], F32, name="result", bufs=3)
+            for t0, t1 in ((0, 512), (512, 768)):
+                bank = psum.tile([P, 512], F32, name="bank_o", bufs=4)
+                matmul(bank[:, 0 : t1 - t0], wq[SHARED, 2], m * P, hs_codes[:, t0:t1], hs_scales[:, t0:t1])
+                nc.vector.tensor_tensor(result[:, t0:t1], bank[:, 0 : t1 - t0], windows[m][:, t0:t1], ADD)
+            nc.sync.dma_start(out[m * P : m * P + P, :], result[:])

import concourse.mybir as mybir

FLOPS = 1845493760

K, T, E, C, H, N = 512, 768, 4, 128, 512, 384
S = E * C
P = 128
J = 4
NT = N // P
SHARED = E

F32 = mybir.dt.float32
BF16 = mybir.dt.bfloat16
U32 = mybir.dt.uint32
U16 = mybir.dt.uint16
U8 = mybir.dt.uint8
FP8X4 = mybir.dt.float8_e4m3fn_x4
SIGMOID = mybir.ActivationFunctionType.Sigmoid
MULT = mybir.AluOpType.mult
ADD = mybir.AluOpType.add

UNITS = ((4, 1), (4, 3), (0, 3), (0, 1), (1, 1), (0, 2), (1, 3), (1, 2), (2, 3), (2, 1), (3, 1), (3, 3), (2, 2), (3, 2), (4, 2))
GATE_AFTER = (2, 3)
S8 = (5, 4, 4, 2, 2, 5, 5, 3, 8, 6, 5, 4, 6, 8, 8)
CHUNK_STEPS = (3, 4, 6, 7, 9, 13)


def tile_moe_shr_glu_sigmoid_kernel(tc, xT, w1, w3, w2, gate, offs, out):
    nc = tc.nc
    with (
        tc.tile_pool(name="keep", bufs=1) as keep,
        tc.tile_pool(name="raws", bufs=1) as raws,
        tc.tile_pool(name="ring", bufs=1) as ring,
        tc.psum_pool(name="psum", bufs=1) as psum,
    ):
        warm = keep.tile([P, 1], F32, name="warm")
        warm_out = keep.tile([P, 1], F32, name="warm_out")
        nc.vector.memset(warm[:], 0.0)
        nc.scalar.activation(warm_out[:], warm[:], SIGMOID)

        offsets = keep.tile([P, S // 16], U16, name="offsets")
        x_view = xT.rearrange("(p j) t -> p j t", j=J)
        x_raw = []
        halves = (slice(0, T // 2), slice(T // 2, T))
        for u in range(2):
            for half in halves:
                raw = keep.tile([P, 2, T // 2], F32, name=f"x_raw{len(x_raw)}")
                nc.sync.dma_start(raw[:], x_view[:, 2 * u : 2 * u + 2, half])
                x_raw.append(raw)
            if u == 0:
                nc.sync.dma_start(offsets[:], offs)

        windows = []
        for m in range(NT):
            window = keep.tile([P, T], F32, name=f"window{m}")
            nc.gpsimd.memset(window[:], 0.0)
            windows.append(window)

        gates = keep.tile([P, NT, S], F32, name="gates")
        raw_w = {}
        for e, layer in UNITS:
            if layer == 2:
                raw = raws.tile([P, J, N], F32, name="raw2", bufs=4)
            else:
                raw = raws.tile([P, J, H], F32, name="raw13", bufs=7)
            source = {1: w1, 3: w3, 2: w2}[layer]
            nc.sync.dma_start(raw[:], source[e, :, :].rearrange("(p j) c -> p j c", j=J))
            raw_w[e, layer] = raw
            if (e, layer) == GATE_AFTER:
                nc.sync.dma_start(gates[:], gate.rearrange("(m p) s -> p m s", p=P))

        def quantize(grouped, codes, scales):
            nc.vector.quantize_mx(out=codes.bitcast(FP8X4), scales=scales, in_=grouped)

        def quantized(name, width):
            codes = keep.tile([P, width], U32, name=f"{name}_codes", align_bytes=64)
            scales = keep.tile([P, width], U8, name=f"{name}_scales", align_bytes=64)
            return codes, scales

        pairs = keep.tile([P, 2, T, 2], BF16, name="pairs", align_bytes=64)
        gathered = keep.tile([P, S * J], BF16, name="gathered", align_bytes=64)
        tokens = keep.tile([P, T * J], BF16, name="tokens", align_bytes=64)
        xg_codes, xg_scales = quantized("xg", S)
        xs_codes, xs_scales = quantized("xs", T)
        for u in range(2):
            for i, half in enumerate(halves):
                dst, src = pairs[:, u, half, :], x_raw[2 * u + i][:].rearrange("p i t -> p t i")
                if "AVAA"[2 * u + i] == "V":
                    nc.vector.tensor_copy(dst, src)
                else:
                    nc.scalar.copy(dst, src)
            words = pairs[:, u, :, :].rearrange("p t i -> p (t i)").bitcast(U32)
            nc.vector.tensor_copy(
                gathered[:].bitcast(U32).rearrange("p (s u) -> p s u", u=2)[:, :, u], words.indirect(offsets[:])
            )
        nc.scalar.copy(
            tokens[:].bitcast(F32).rearrange("p (t u) -> p t u", u=2),
            pairs[:].rearrange("p u t i -> p (u t i)").bitcast(F32).rearrange("p (u t) -> p t u", u=2),
        )
        quantize(gathered[:], xg_codes[:], xg_scales[:])
        for t0, t1 in ((0, 512), (512, 768)):
            quantize(tokens[:, t0 * J : t1 * J], xs_codes[:, t0:t1], xs_scales[:, t0:t1])

        wq, views = {}, {}

        def cast_views(unit):
            e, layer = unit
            if layer == 2:
                grouped = ring.tile([P, N * J], BF16, name="grouped2", bufs=3, align_bytes=64)
                dst = grouped[:].rearrange("p (c i j) -> p c j i", i=4, j=J)
                src = raw_w[unit][:].rearrange("p j (c i) -> p c j i", i=4)
                cut = S8[UNITS.index(unit)] * 12
            else:
                grouped = ring.tile([P, H * J], BF16, name="grouped13", bufs=4, align_bytes=64)
                dst = grouped[:].rearrange("p (t m j) -> p m j t", t=J, j=J)
                src = raw_w[unit][:].rearrange("p j (m t) -> p m j t", t=J)
                cut = S8[UNITS.index(unit)] * 16
            views[unit] = grouped, dst, src, cut

        def cast_scalar(unit):
            cast_views(unit)
            grouped, dst, src, cut = views[unit]
            if cut > 0:
                nc.scalar.copy(dst[:, 0:cut], src[:, 0:cut])

        def cast_vector(unit):
            grouped, dst, src, cut = views[unit]
            if cut < dst.shape[1]:
                nc.vector.tensor_copy(dst[:, cut:], src[:, cut:])

        def quantize_weights(unit):
            e, layer = unit
            grouped = views[unit][0]
            width, cuts = (N, (0, 256, 384)) if layer == 2 else (H, (0, 512))
            codes, scales = wq[unit] = quantized(f"w{layer}_{e}", width)
            for n0, n1 in zip(cuts[:-1], cuts[1:]):
                quantize(grouped[:, n0 * J : n1 * J], codes[:, n0:n1], scales[:, n0:n1])

        def matmul(dst, weights, column, codes, scales):
            nc.tensor.matmul_mx(
                out=dst,
                lhsT=weights[0][:, column : column + P].bitcast(FP8X4),
                lhsT_scale=weights[1][:, column : column + P],
                rhs=codes.bitcast(FP8X4),
                rhs_scale=scales,
                start=True,
                stop=True,
            )

        h_codes, h_scales = quantized("h", S)
        hs_codes, hs_scales = quantized("hs", T)
        banks, sigs, hiddens = {}, {}, {}

        def multiply_first(chunk):
            e, c = chunk
            cols = slice(c * C, c * C + C)
            codes, scales = (xs_codes, xs_scales) if e == SHARED else (xg_codes, xg_scales)
            for layer, tag in ((1, "bank_a"), (3, "bank_b")):
                bank = psum.tile([P, J, C], F32, name=tag, bufs=2)
                for t in range(J):
                    matmul(bank[:, t, :], wq[e, layer], t * P, codes[:, cols], scales[:, cols])
                banks[chunk, layer] = bank

        def sigmoid(chunk):
            sig = ring.tile([P, C, J], F32, name="sig", bufs=3)
            nc.scalar.activation(sig[:], banks[chunk, 1][:].rearrange("p t n -> p n t"), SIGMOID)
            sigs[chunk] = sig

        def product(chunk):
            e, c = chunk
            if e == SHARED and c % 2 == 1:
                hidden, at = hiddens[e, c - 1][0], C * J
            else:
                width = 2 if e == SHARED else 1
                hidden, at = ring.tile([P, width * C * J], BF16, name=f"hidden{width}", bufs=2, align_bytes=64), 0
            nc.vector.tensor_tensor(
                hidden[:, at : at + C * J].rearrange("p (n t) -> p n t", t=J),
                banks[chunk, 3][:].rearrange("p t n -> p n t"),
                sigs[chunk][:],
                MULT,
            )
            hiddens[chunk] = hidden, at

        def quantize_hidden(chunk):
            e, c = chunk
            if e == SHARED and c % 2 == 0:
                return
            first = c - 1 if e == SHARED else c
            cols = slice(first * C, c * C + C)
            codes, scales = (hs_codes, hs_scales) if e == SHARED else (h_codes, h_scales)
            quantize(hiddens[chunk][0][:], codes[:, cols], scales[:, cols])

        def multiply_second(e):
            cols = slice(e * C, e * C + C)
            bank = psum.tile([P, 512], F32, name="bank_o", bufs=4)
            for m in range(NT):
                matmul(bank[:, m * P : m * P + P], wq[e, 2], m * P, h_codes[:, cols], h_scales[:, cols])
            banks[e] = bank

        routeds = {}

        def copy_routed(e):
            routed = ring.tile([P, N], F32, name="routed", bufs=2)
            nc.scalar.copy(routed[:], banks[e][:, 0:N])
            routeds[e] = routed

        def scatter(e):
            for m in range(NT):
                nc.vector.tensor_tensor(
                    windows[m][:].indirect(offsets[:, e * 8 : e * 8 + 8]),
                    routeds[e][:, m * P : m * P + P],
                    gates[:, m, e * C : e * C + C],
                    MULT,
                )

        step_of = {unit: k for k, unit in enumerate(UNITS)}
        chunk_step = {(SHARED, c): k for c, k in enumerate(CHUNK_STEPS)}
        second_step = {}
        for e in range(E):
            chunk_step[e, e] = max(step_of[e, 1], step_of[e, 3]) + 2
            second_step[e] = max(chunk_step[e, e] + 2, step_of[e, 2] + 2)
        for k in range(len(UNITS) + 4):
            started = [chunk for chunk, step in chunk_step.items() if step == k]
            before = [chunk for chunk, step in chunk_step.items() if step == k - 1]
            seconds = [e for e, step in second_step.items() if step == k]
            for e in seconds:
                multiply_second(e)
            for chunk in started:
                multiply_first(chunk)
            for chunk in before:
                product(chunk)
            if k < len(UNITS):
                cast_scalar(UNITS[k])
            for e in seconds:
                copy_routed(e)
            for chunk in started:
                sigmoid(chunk)
            if k < len(UNITS):
                cast_vector(UNITS[k])
            if 1 <= k <= len(UNITS):
                quantize_weights(UNITS[k - 1])
            for chunk in before:
                quantize_hidden(chunk)
            for e, step in second_step.items():
                if step == k - 1:
                    scatter(e)

        for m in range(NT):
            result = ring.tile([P, T], F32, name="result", bufs=3)
            for t0, t1 in ((0, 512), (512, 768)):
                bank = psum.tile([P, 512], F32, name="bank_o", bufs=4)
                matmul(bank[:, 0 : t1 - t0], wq[SHARED, 2], m * P, hs_codes[:, t0:t1], hs_scales[:, t0:t1])
                nc.vector.tensor_tensor(result[:, t0:t1], bank[:, 0 : t1 - t0], windows[m][:, t0:t1], ADD)
            nc.sync.dma_start(out[m * P : m * P + P, :], result[:])
